import numpy as np
import ml_dtypes


def mxq(x, axis, fmt="e4m3"):
    dtype, down = {"e4m3": (ml_dtypes.float8_e4m3fn, 7), "e5m2": (ml_dtypes.float8_e5m2, 14)}[fmt]
    v = np.moveaxis(np.asarray(x, np.float32).astype(ml_dtypes.bfloat16).astype(np.float64), axis, -1)
    blocks = v.reshape(v.shape[:-1] + (-1, 32))
    amax = np.abs(blocks).max(-1, keepdims=True)
    byte = np.maximum(np.where(amax > 0, np.frexp(amax)[1] - 1 + 127, 0) - down, 1)
    scale = np.exp2(byte - 127.0)
    codes = (blocks / scale).astype(np.float32).astype(dtype).astype(np.float64)
    return np.moveaxis((codes * scale).reshape(v.shape), -1, axis)


WIDE = False


def mx_kscale(k):
    if not WIDE:
        return np.ones(k)
    levels = np.array([10, -10, 5, -5, 0])
    if k % 512:
        return np.exp2(np.random.permutation(np.resize(levels, k // 32))).repeat(32)
    a = np.empty((k // 512, 16))
    for p in range(k // 512):
        a[p, :8] = np.random.permutation(np.resize(levels, 8))
        for g in range(8):
            far = levels[np.abs(levels - a[p, g]) >= 10]
            a[p, g + 8] = far[np.random.randint(len(far))]
    return np.exp2(a.ravel()).repeat(32)


def f64(x):
    return np.asarray(x).astype(np.float64)


def striped(idx):
    return np.tile(idx.reshape(-1, 16).T, (8, 1)).astype(np.uint16)


def unstriped(offs):
    return offs[:16].T.reshape(-1).astype(np.int64)


E2M1 = np.array([0.0, 0.5, 1.0, 1.5, 2.0, 3.0, 4.0, 6.0, -0.0, -0.5, -1.0, -1.5, -2.0, -3.0, -4.0, -6.0])


def pack_weight(w, fmt):
    k, n = w.shape
    w = f64(np.asarray(w, np.float32).astype(ml_dtypes.bfloat16)).reshape(k // 32, 32, n)
    amax = np.abs(w).max(1)
    if fmt == "e4m3":
        byte = np.frexp(amax)[1] - 1 + 127 - 7
    else:
        mant, ex = np.frexp(amax / 6.0)
        byte = np.where(mant > 0.5, ex, ex - 1) + 127
    byte = np.clip(np.where(amax > 0, byte, 1), 1, 254)
    scaled = (w * np.exp2(127.0 - byte)[:, None, :]).reshape(k, n).astype(np.float32)
    by_word = np.ascontiguousarray(scaled.reshape(k // 512, 128, 4, n).transpose(0, 1, 3, 2))
    if fmt == "e4m3":
        words = by_word.astype(ml_dtypes.float8_e4m3fn).view(np.uint8)
    else:
        c = by_word.astype(ml_dtypes.float4_e2m1fn).view(np.uint8) & 0xF
        words = (c[..., 0::2] | (c[..., 1::2] << 4)).reshape(k // 512, 128, 2 * n)
    return np.ascontiguousarray(words), np.ascontiguousarray(byte.astype(np.uint8).reshape(k // 512, 16, n))


def unpack_weight(words, scales, fmt):
    g, _, n = scales.shape
    words = np.ascontiguousarray(words).reshape(g, 128, n, -1)
    if fmt == "e4m3":
        vals = words.view(ml_dtypes.float8_e4m3fn).astype(np.float64)
    else:
        nib = np.empty((g, 128, n, 4), np.uint8)
        nib[..., 0::2] = words & 0xF
        nib[..., 1::2] = words >> 4
        vals = E2M1[nib]
    vals = vals * np.repeat(np.exp2(scales.astype(np.float64) - 127.0), 8, axis=1)[..., None]
    return vals.transpose(0, 1, 3, 2).reshape(g * 512, n)


def sigmoid(v):
    return 1.0 / (1.0 + np.exp(-np.maximum(v, -700.0)))


def d_sigmoid(v):
    s = 1.0 / (1.0 + np.exp(-np.maximum(v, -700.0)))
    return s * (1.0 - s)


K, T, E, C, H, N = 256, 768, 4, 128, 1024, 512


def by_expert(wq, xq):
    return np.concatenate([wq[e].T @ xq[:, e * C:(e + 1) * C] for e in range(E)], axis=1)


def setup_inputs():
    n = np.random.standard_normal
    s = mx_kscale(N)[:, None]
    u = mx_kscale(H)
    w2 = [pack_weight(m, "e2m1") for m in n((E, N, H)) / np.sqrt(N) / s[None] * u[None, None, :]]
    w1 = [pack_weight(m, "e2m1") for m in n((E, H, K)) / np.sqrt(H) / u[None, :, None]]
    w3 = [pack_weight(m, "e2m1") for m in n((E, H, K)) / np.sqrt(H) / u[None, :, None]]
    return {
        "dyT": (n((N, T)) * s).astype(np.float32),
        "a1": n((H, E * C)).astype(np.float32),
        "a3": n((H, E * C)).astype(np.float32),
        "w2_words": np.stack([m[0] for m in w2]),
        "w2_scales": np.stack([m[1] for m in w2]),
        "w1_words": np.stack([m[0] for m in w1]),
        "w1_scales": np.stack([m[1] for m in w1]),
        "w3_words": np.stack([m[0] for m in w3]),
        "w3_scales": np.stack([m[1] for m in w3]),
        "gate": np.tile(np.random.uniform(0.2, 1.0, E * C), (N, 1)).astype(np.float32),
        "offs": striped(np.random.permutation(T)[:E * C]),
    }


def reference(dyT, a1, a3, w2_words, w2_scales, w1_words, w1_scales, w3_words, w3_scales, gate, offs):
    idx = unstriped(offs)
    w2 = np.stack([unpack_weight(w2_words[e], w2_scales[e], "e2m1") for e in range(E)])
    w1 = np.stack([unpack_weight(w1_words[e], w1_scales[e], "e2m1") for e in range(E)])
    w3 = np.stack([unpack_weight(w3_words[e], w3_scales[e], "e2m1") for e in range(E)])
    gq = mxq(f64(gate) * f64(dyT)[:, idx], 0, "e4m3")
    dh = by_expert(w2, gq)
    da1 = dh * f64(a3) * d_sigmoid(f64(a1))
    da3 = dh * sigmoid(f64(a1))
    dx = by_expert(w1, mxq(da1, 0, "e4m3")) + by_expert(w3, mxq(da3, 0, "e4m3"))
    out = np.zeros((K, T))
    out[:, idx] = dx
    return out

@@ -1,0 +1,249 @@
+from contextlib import ExitStack
+
+import concourse.mybir as mybir
+from concourse.masks import make_identity
+
+N, T, E, C, H, K = 512, 768, 4, 128, 1024, 256
+SLOTS = E * C
+P = 128
+
+FLOPS = 2 * SLOTS * H * (N + 2 * K)
+BYTES = 4 * (N * T + 2 * H * SLOTS + P * SLOTS + K * T) + 2 * P * SLOTS // 16 + E * (N * H + 2 * H * K) * 17 // 32
+
+F32 = mybir.dt.float32
+BF16 = mybir.dt.bfloat16
+I32 = mybir.dt.int32
+U32 = mybir.dt.uint32
+U16 = mybir.dt.uint16
+U8 = mybir.dt.uint8
+FP8X4 = mybir.dt.float8_e4m3fn_x4
+FP4X4 = mybir.dt.float4_e2m1fn_x4
+MULT = mybir.AluOpType.mult
+SIGMOID = mybir.ActivationFunctionType.Sigmoid
+
+
+def tile_moe_bdx_glu_sigmoid_kernel(
+    tc, dyT, a1, a3, w2_words, w2_scales, w1_words, w1_scales, w3_words, w3_scales, gate, offs, out
+):
+    nc = tc.nc
+    with ExitStack() as ctx:
+        keep = ctx.enter_context(tc.tile_pool(name="keep", bufs=1))
+        ring = ctx.enter_context(tc.tile_pool(name="ring", bufs=3))
+        psum = ctx.enter_context(tc.psum_pool(name="psum", bufs=2))
+
+        offsets = keep.tile([P, SLOTS // 16], U16, name="offsets")
+        dy = [keep.tile([P, T], F32, name="dy%d" % t) for t in range(4)]
+        gates = keep.tile([P, SLOTS], F32, name="gates")
+        g4 = keep.tile([P, 4, SLOTS], F32, name="g4")
+        g_bf = keep.tile([P, SLOTS, 4], BF16, name="g_bf", align_bytes=64)
+        g_codes = keep.tile([P, SLOTS], U32, name="g_codes", align_bytes=64)
+        g_scales = keep.tile([P, SLOTS], U8, name="g_scales", align_bytes=64)
+        w2 = keep.tile([P, E, 2 * H], U8, name="w2", align_bytes=64)
+        w2_plane = keep.tile([P, E, H], U8, name="w2_plane", align_bytes=64)
+        w13 = keep.tile([P, 2, 2 * E, 2 * K], U8, name="w13", align_bytes=64)
+        w13_plane = keep.tile([P, 2, 2 * E, K], U8, name="w13_plane", align_bytes=64)
+        ident = keep.tile([P, P], F32, name="ident")
+        windows = [keep.tile([P, T], F32, name="window%d" % kt) for kt in range(2)]
+        warm = keep.tile([P, 1], F32, name="warm")
+        saved = {}
+        for name in ("a1", "a3", "sig", "nsig", "v"):
+            for pair in range(2):
+                for s in range(2):
+                    saved[name, pair, s] = keep.tile([P, 4, 2 * C], F32, name="%s_%d%d" % (name, pair, s))
+
+        def load_saved(name, src, pair, s):
+            nc.sync.dma_start(
+                out=saved[name, pair, s][:],
+                in_=src[512 * s : 512 * (s + 1), 2 * C * pair : 2 * C * (pair + 1)].rearrange("(p t) j -> p t j", t=4),
+            )
+
+        dy_rows = dyT.rearrange("(p t) j -> p t j", t=4)
+        nc.sync.dma_start(offsets[:], offs)
+        nc.scalar.dma_start(out=gates[:], in_=gate[0:P, :])
+        for t in range(4):
+            nc.sync.dma_start(out=dy[t][:], in_=dy_rows[:, t, :])
+
+        nc.vector.memset(warm[:], 0.0)
+        nc.scalar.activation(warm[:], warm[:], SIGMOID)
+        nc.vector.memset(w2_plane[:].rearrange("p e i -> p (e i)").bitcast(I32), 0)
+        nc.vector.memset(w13_plane[:].rearrange("p a g k -> p (a g k)").bitcast(I32), 0)
+        make_identity(nc, ident[:])
+        for kt in range(2):
+            nc.gpsimd.memset(windows[kt][:], 0.0)
+
+        w2_src = w2_words.bitcast(I32)
+        w2_scale_src = w2_scales.bitcast(I32).rearrange("e s f i -> f (e s) i")
+        w2_dst = w2[:].rearrange("p e i -> p (e i)").bitcast(I32).rearrange("p (e i) -> p e i", e=E)
+        w2_plane_dst = w2_plane[:].rearrange("p e i -> p (e i)").bitcast(I32).rearrange("p (e i) -> p e i", e=E)
+        for quad in range(4):
+            nc.scalar.dma_start(
+                out=w2_plane_dst[32 * quad : 32 * quad + 4, :, :],
+                in_=w2_scale_src[4 * quad : 4 * quad + 4, :, :],
+            )
+        load_saved("a1", a1, 0, 0)
+        nc.sync.dma_start(out=w2_dst[:, 0:2, :], in_=w2_src[0:2, 0, :, :].rearrange("e p i -> p e i"))
+        load_saved("a3", a3, 0, 0)
+        load_saved("a1", a1, 0, 1)
+        load_saved("a3", a3, 0, 1)
+        w13_dst = w13[:].rearrange("p a g k -> p (a g k)").bitcast(I32).rearrange("p (a g k) -> p a g k", a=2, g=2 * E)
+        w13_plane_dst = (
+            w13_plane[:].rearrange("p a g k -> p (a g k)").bitcast(I32).rearrange("p (a g k) -> p a g k", a=2, g=2 * E)
+        )
+        for a, words, scales in ((0, w3_words, w3_scales), (1, w1_words, w1_scales)):
+            scale_src = scales.bitcast(I32).rearrange("e s f k -> f (e s) k")
+            for quad in range(4):
+                nc.sync.dma_start(
+                    out=w13_plane_dst[32 * quad : 32 * quad + 4, a, :, :],
+                    in_=scale_src[4 * quad : 4 * quad + 4, :, :],
+                )
+            nc.sync.dma_start(out=w13_dst[:, a, :, :], in_=words.bitcast(I32).rearrange("e s p k -> p (e s) k"))
+        nc.sync.dma_start(out=w2_dst[:, 2:4, :], in_=w2_src[2:4, 0, :, :].rearrange("e p i -> p e i"))
+        for s in range(2):
+            load_saved("a1", a1, 1, s)
+            load_saved("a3", a3, 1, s)
+
+        def gather(t, j0, j1):
+            nc.vector.tensor_tensor(
+                g4[:, t, j0:j1], dy[t][:].indirect(offsets[:, j0 // 16 : j1 // 16]), gates[:, j0:j1], MULT
+            )
+
+        def interleave(e, copy):
+            copy(
+                out=g_bf[:, C * e : C * (e + 1), :], in_=g4[:, :, C * e : C * (e + 1)].rearrange("p t j -> p j t")
+            )
+
+        def quantize_g(e):
+            cols = slice(C * e, C * (e + 1))
+            nc.vector.quantize_mx(
+                out=g_codes[:, cols].bitcast(FP8X4),
+                scales=g_scales[:, cols],
+                in_=g_bf[:, cols, :].rearrange("p j t -> p (j t)"),
+            )
+
+        turned = {}
+        codes = {}
+
+        def first_product(e, s):
+            dhT = psum.tile([P, 512], F32, name="dhT")
+            nc.tensor.matmul_mx(
+                out=dhT[:],
+                lhsT=g_codes[:, C * e : C * (e + 1)].bitcast(FP8X4),
+                lhsT_scale=g_scales[:, C * e : C * (e + 1)],
+                rhs=w2[:, e, 1024 * s : 1024 * (s + 1)].bitcast(FP4X4),
+                rhs_scale=w2_plane[:, e, 512 * s : 512 * (s + 1)],
+                start=True,
+                stop=True,
+            )
+            dhT_sb = ring.tile([P, 4, P], F32, name="dhT_sb")
+            nc.scalar.copy(out=dhT_sb[:], in_=dhT[:].rearrange("j (m t) -> j t m", t=4))
+            dh = psum.tile([P, 4, P], F32, name="dh", bufs=4)
+            for t in range(4):
+                nc.tensor.transpose(dh[:, t, :], dhT_sb[:, t, :], ident[:])
+            turned[e, s] = dh
+
+        def factors(pair, s, j0, j1):
+            get = lambda name: saved[name, pair, s][:, :, j0:j1]
+            nc.scalar.activation(get("sig"), get("a1"), SIGMOID)
+            nc.scalar.activation(get("nsig"), get("a1"), SIGMOID, scale=-1.0)
+
+        def factor_products(pair, s, j0, j1):
+            get = lambda name: saved[name, pair, s][:, :, j0:j1]
+            nc.gpsimd.tensor_tensor(get("v"), get("nsig"), get("a3"), MULT)
+
+        def saved_factor(name, e, s):
+            pair, h = divmod(e, 2)
+            return saved[name, pair, s][:, :, C * h : C * (h + 1)].rearrange("p t j -> p j t")
+
+        da3_sums = {}
+        das = {}
+
+        def product_da3(e, s):
+            da3 = ring.tile([P, C, 4], F32, name="da3", bufs=4)
+            da = ring.tile([P, 2, C, 4], BF16, name="da", align_bytes=64, bufs=4)
+            nc.vector.tensor_tensor(da3[:], turned[e, s][:].rearrange("p t j -> p j t"), saved_factor("sig", e, s), MULT)
+            nc.scalar.copy(out=da[:, 0, :, :], in_=da3[:])
+            da3_sums[e, s] = da3
+            das[e, s] = da
+
+        def product_da1(e, s):
+            nc.vector.tensor_tensor(das[e, s][:, 1, :, :], da3_sums[e, s][:], saved_factor("v", e, s), MULT)
+
+        def quantize_da(e, s):
+            da = das[e, s]
+            words = ring.tile([P, 2 * C], U32, name="da_codes", align_bytes=64, bufs=4)
+            scales = ring.tile([P, 2 * C], U8, name="da_scales", align_bytes=64, bufs=4)
+            nc.vector.quantize_mx(
+                out=words[:].bitcast(FP8X4), scales=scales[:], in_=da[:].rearrange("p a j t -> p (a j t)")
+            )
+            codes[e, s] = (words, scales)
+
+        def second_product(e):
+            dx = psum.tile([P, 2, C], F32, name="dx")
+            for kt in range(2):
+                for s in range(2):
+                    for a in range(2):
+                        words, scales = codes[e, s]
+                        nc.tensor.matmul_mx(
+                            out=dx[:, kt, :],
+                            lhsT=w13[:, a, 2 * e + s, 256 * kt : 256 * (kt + 1)].bitcast(FP4X4),
+                            lhsT_scale=w13_plane[:, a, 2 * e + s, P * kt : P * (kt + 1)],
+                            rhs=words[:, C * a : C * (a + 1)].bitcast(FP8X4),
+                            rhs_scale=scales[:, C * a : C * (a + 1)],
+                            start=(s == 0 and a == 0),
+                            stop=(s == 1 and a == 1),
+                        )
+            dx_sb = ring.tile([P, 2, C], F32, name="dx_sb")
+            nc.scalar.copy(out=dx_sb[:], in_=dx[:])
+            return dx_sb
+
+        def scatter(e, dx_sb):
+            for kt in range(2):
+                nc.vector.tensor_copy(windows[kt][:].indirect(offsets[:, 8 * e : 8 * (e + 1)]), dx_sb[:, kt, :])
+
+        steps = [(e, s) for e in range(E) for s in range(2)]
+
+        def prepare(i):
+            if i < len(steps):
+                e, s = steps[i]
+                pair, h = divmod(e, 2)
+                factors(pair, s, C * h, C * (h + 1))
+                factor_products(pair, s, C * h, C * (h + 1))
+
+        for t in range(3):
+            gather(t, 0, SLOTS)
+        gather(3, 0, C)
+        gather(3, C, 2 * C)
+        interleave(0, nc.vector.tensor_copy)
+        gather(3, 2 * C, SLOTS)
+        quantize_g(0)
+        interleave(1, nc.vector.tensor_copy)
+        first_product(0, 0)
+        first_product(0, 1)
+        for e in range(2, E):
+            interleave(e, nc.scalar.copy)
+        quantize_g(1)
+        prepare(0)
+        prepare(1)
+        quantize_g(2)
+        quantize_g(3)
+        prepare(2)
+        product_da3(*steps[0])
+        dxs = {}
+        for i in range(len(steps)):
+            e, s = steps[i]
+            if i + 2 < len(steps):
+                first_product(*steps[i + 2])
+            prepare(i + 3)
+            if i + 1 < len(steps):
+                product_da3(*steps[i + 1])
+            if i >= 1:
+                quantize_da(*steps[i - 1])
+            product_da1(e, s)
+            if s == 0 and e >= 1:
+                dxs[e - 1] = second_product(e - 1)
+            if s == 1 and e >= 1:
+                scatter(e - 1, dxs[e - 1])
+        quantize_da(*steps[-1])
+        scatter(E - 1, second_product(E - 1))
+        for kt in range(2):
+            nc.sync.dma_start(out=out[P * kt : P * (kt + 1), :], in_=windows[kt][:])

@@ -19,7 +19,9 @@ U8 = mybir.dt.uint8
 FP8X4 = mybir.dt.float8_e4m3fn_x4
 FP4X4 = mybir.dt.float4_e2m1fn_x4
 MULT = mybir.AluOpType.mult
+SUBTRACT = mybir.AluOpType.subtract
 SIGMOID = mybir.ActivationFunctionType.Sigmoid
+SQUARE = mybir.ActivationFunctionType.Square
 
 
 def tile_moe_bdx_glu_sigmoid_kernel(
@@ -45,11 +47,17 @@ def tile_moe_bdx_glu_sigmoid_kernel(
         ident = keep.tile([P, P], F32, name="ident")
         windows = [keep.tile([P, T], F32, name="window%d" % kt) for kt in range(2)]
         warm = keep.tile([P, 1], F32, name="warm")
+        minus_half = keep.tile([P, 1], F32, name="minus_half")
         saved = {}
-        for name in ("a1", "a3", "sig", "nsig", "v"):
+        for name in ("a1", "a3"):
             for pair in range(2):
                 for s in range(2):
                     saved[name, pair, s] = keep.tile([P, 4, 2 * C], F32, name="%s_%d%d" % (name, pair, s))
+
+        for name in ("sig", "sq", "nq"):
+            for e in range(E):
+                for s in range(2):
+                    saved[name, e, s] = keep.tile([P, C, 4], F32, name="%s_%d%d" % (name, e, s))
 
         def load_saved(name, src, pair, s):
             nc.sync.dma_start(
@@ -64,6 +72,7 @@ def tile_moe_bdx_glu_sigmoid_kernel(
             nc.sync.dma_start(out=dy[t][:], in_=dy_rows[:, t, :])
 
         nc.vector.memset(warm[:], 0.0)
+        nc.vector.memset(minus_half[:], -0.5)
         nc.scalar.activation(warm[:], warm[:], SIGMOID)
         nc.vector.memset(w2_plane[:].rearrange("p e i -> p (e i)").bitcast(I32), 0)
         nc.vector.memset(w13_plane[:].rearrange("p a g k -> p (a g k)").bitcast(I32), 0)
@@ -141,32 +150,27 @@ def tile_moe_bdx_glu_sigmoid_kernel(
                 nc.tensor.transpose(dh[:, t, :], dhT_sb[:, t, :], ident[:])
             turned[e, s] = dh
 
-        def factors(pair, s, j0, j1):
-            get = lambda name: saved[name, pair, s][:, :, j0:j1]
-            nc.scalar.activation(get("sig"), get("a1"), SIGMOID)
-            nc.scalar.activation(get("nsig"), get("a1"), SIGMOID, scale=-1.0)
-
-        def factor_products(pair, s, j0, j1):
-            get = lambda name: saved[name, pair, s][:, :, j0:j1]
-            nc.gpsimd.tensor_tensor(get("v"), get("nsig"), get("a3"), MULT)
-
-        def saved_factor(name, e, s):
+        def saved_slice(name, e, s):
             pair, h = divmod(e, 2)
             return saved[name, pair, s][:, :, C * h : C * (h + 1)].rearrange("p t j -> p j t")
 
-        da3_sums = {}
+        def factors(e, s):
+            nc.scalar.activation(saved["sig", e, s][:], saved_slice("a1", e, s), SIGMOID)
+            nc.scalar.activation(saved["sq", e, s][:], saved["sig", e, s][:], SQUARE, bias=minus_half[:])
+
+        def factor_products(e, s):
+            nc.vector.scalar_tensor_tensor(
+                saved["nq", e, s][:], saved["sq", e, s][:], 0.25, saved_slice("a3", e, s), SUBTRACT, MULT
+            )
+
         das = {}
 
-        def product_da3(e, s):
-            da3 = ring.tile([P, C, 4], F32, name="da3", bufs=4)
-            da = ring.tile([P, 2, C, 4], BF16, name="da", align_bytes=64, bufs=4)
-            nc.vector.tensor_tensor(da3[:], turned[e, s][:].rearrange("p t j -> p j t"), saved_factor("sig", e, s), MULT)
-            nc.scalar.copy(out=da[:, 0, :, :], in_=da3[:])
-            da3_sums[e, s] = da3
+        def product_da(e, s):
+            da = ring.tile([P, 2, C, 4], BF16, name="da", align_bytes=64)
+            dh = turned[e, s][:].rearrange("p t j -> p j t")
+            nc.vector.tensor_tensor(da[:, 0, :, :], dh, saved["sig", e, s][:], MULT)
+            nc.vector.scalar_tensor_tensor(da[:, 1, :, :], dh, -1.0, saved["nq", e, s][:], MULT, MULT)
             das[e, s] = da
-
-        def product_da1(e, s):
-            nc.vector.tensor_tensor(das[e, s][:, 1, :, :], da3_sums[e, s][:], saved_factor("v", e, s), MULT)
 
         def quantize_da(e, s):
             da = das[e, s]
@@ -201,14 +205,6 @@ def tile_moe_bdx_glu_sigmoid_kernel(
                 nc.vector.tensor_copy(windows[kt][:].indirect(offsets[:, 8 * e : 8 * (e + 1)]), dx_sb[:, kt, :])
 
         steps = [(e, s) for e in range(E) for s in range(2)]
-
-        def prepare(i):
-            if i < len(steps):
-                e, s = steps[i]
-                pair, h = divmod(e, 2)
-                factors(pair, s, C * h, C * (h + 1))
-                factor_products(pair, s, C * h, C * (h + 1))
-
         for t in range(3):
             gather(t, 0, SLOTS)
         gather(3, 0, C)
@@ -222,28 +218,28 @@ def tile_moe_bdx_glu_sigmoid_kernel(
         for e in range(2, E):
             interleave(e, nc.scalar.copy)
         quantize_g(1)
-        prepare(0)
-        prepare(1)
+        factors(0, 0)
+        factor_products(0, 0)
+        factors(0, 1)
+        factor_products(0, 1)
         quantize_g(2)
         quantize_g(3)
-        prepare(2)
-        product_da3(*steps[0])
+        factors(1, 0)
         dxs = {}
         for i in range(len(steps)):
             e, s = steps[i]
             if i + 2 < len(steps):
                 first_product(*steps[i + 2])
-            prepare(i + 3)
-            if i + 1 < len(steps):
-                product_da3(*steps[i + 1])
-            if i >= 1:
-                quantize_da(*steps[i - 1])
-            product_da1(e, s)
-            if s == 0 and e >= 1:
-                dxs[e - 1] = second_product(e - 1)
-            if s == 1 and e >= 1:
-                scatter(e - 1, dxs[e - 1])
-        quantize_da(*steps[-1])
-        scatter(E - 1, second_product(E - 1))
+            if i + 3 < len(steps):
+                factors(*steps[i + 3])
+            product_da(e, s)
+            if i + 2 < len(steps):
+                factor_products(*steps[i + 2])
+            quantize_da(e, s)
+            if s == 1:
+                dxs[e] = second_product(e)
+                if e >= 1:
+                    scatter(e - 1, dxs[e - 1])
+        scatter(E - 1, dxs[E - 1])
         for kt in range(2):
             nc.sync.dma_start(out=out[P * kt : P * (kt + 1), :], in_=windows[kt][:])

@@ -50,66 +50,82 @@ def tile_moe_bdx_glu_sigmoid_kernel(
         minus_half = keep.tile([P, 1], F32, name="minus_half")
         saved = {}
         for name in ("a1", "a3"):
-            for pair in range(2):
-                for s in range(2):
-                    saved[name, pair, s] = keep.tile([P, 4, 2 * C], F32, name="%s_%d%d" % (name, pair, s))
-
+            for half in range(2):
+                saved[name, 0, half] = keep.tile([P, 4, 2 * C], F32, name="%s_0%d" % (name, half))
+            saved[name, 1] = keep.tile([P, 4, SLOTS], F32, name="%s_1" % name)
         for name in ("sig", "sq", "nq"):
             for e in range(E):
                 for s in range(2):
                     saved[name, e, s] = keep.tile([P, C, 4], F32, name="%s_%d%d" % (name, e, s))
 
-        def load_saved(name, src, pair, s):
+        sources = {"a1": a1, "a3": a3}
+
+        def load_first_half(name, half):
             nc.sync.dma_start(
-                out=saved[name, pair, s][:],
-                in_=src[512 * s : 512 * (s + 1), 2 * C * pair : 2 * C * (pair + 1)].rearrange("(p t) j -> p t j", t=4),
+                out=saved[name, 0, half][:],
+                in_=sources[name][0:512, 2 * C * half : 2 * C * (half + 1)].rearrange("(p t) j -> p t j", t=4),
             )
 
-        dy_rows = dyT.rearrange("(p t) j -> p t j", t=4)
-        nc.sync.dma_start(offsets[:], offs)
-        nc.scalar.dma_start(out=gates[:], in_=gate[0:P, :])
-        for t in range(4):
-            nc.sync.dma_start(out=dy[t][:], in_=dy_rows[:, t, :])
-
-        nc.vector.memset(warm[:], 0.0)
-        nc.vector.memset(minus_half[:], -0.5)
-        nc.scalar.activation(warm[:], warm[:], SIGMOID)
-        nc.vector.memset(w2_plane[:].rearrange("p e i -> p (e i)").bitcast(I32), 0)
-        nc.vector.memset(w13_plane[:].rearrange("p a g k -> p (a g k)").bitcast(I32), 0)
-        make_identity(nc, ident[:])
-        for kt in range(2):
-            nc.gpsimd.memset(windows[kt][:], 0.0)
+        def load_second_half(name):
+            nc.sync.dma_start(
+                out=saved[name, 1][:], in_=sources[name][512:1024, :].rearrange("(p t) j -> p t j", t=4)
+            )
 
         w2_src = w2_words.bitcast(I32)
         w2_scale_src = w2_scales.bitcast(I32).rearrange("e s f i -> f (e s) i")
         w2_dst = w2[:].rearrange("p e i -> p (e i)").bitcast(I32).rearrange("p (e i) -> p e i", e=E)
         w2_plane_dst = w2_plane[:].rearrange("p e i -> p (e i)").bitcast(I32).rearrange("p (e i) -> p e i", e=E)
+        w13_dst = w13[:].rearrange("p a g k -> p (a g k)").bitcast(I32).rearrange("p (a g k) -> p a g k", a=2, g=2 * E)
+        w13_plane_dst = (
+            w13_plane[:].rearrange("p a g k -> p (a g k)").bitcast(I32).rearrange("p (a g k) -> p a g k", a=2, g=2 * E)
+        )
+
+        def load_w2(e):
+            nc.sync.dma_start(out=w2_dst[:, e, :], in_=w2_src[e, 0, :, :])
+
+        dy_rows = dyT.rearrange("(p t) j -> p t j", t=4)
+
+        def load_dy(t):
+            nc.sync.dma_start(out=dy[t][:], in_=dy_rows[:, t, :])
+
+        nc.sync.dma_start(offsets[:], offs)
+        nc.scalar.dma_start(out=gates[:], in_=gate[0:P, :])
+        nc.vector.memset(w2_plane[:].rearrange("p e i -> p (e i)").bitcast(I32), 0)
+        nc.vector.memset(minus_half[:], -0.5)
+        nc.vector.memset(warm[:], 0.0)
+        nc.scalar.activation(warm[:], warm[:], SIGMOID)
+        nc.vector.memset(w13_plane[:].rearrange("p a g k -> p (a g k)").bitcast(I32), 0)
+        make_identity(nc, ident[:])
+        for kt in range(2):
+            nc.gpsimd.memset(windows[kt][:], 0.0)
         for quad in range(4):
             nc.scalar.dma_start(
                 out=w2_plane_dst[32 * quad : 32 * quad + 4, :, :],
                 in_=w2_scale_src[4 * quad : 4 * quad + 4, :, :],
             )
-        load_saved("a1", a1, 0, 0)
-        nc.sync.dma_start(out=w2_dst[:, 0:2, :], in_=w2_src[0:2, 0, :, :].rearrange("e p i -> p e i"))
-        load_saved("a3", a3, 0, 0)
-        load_saved("a1", a1, 0, 1)
-        load_saved("a3", a3, 0, 1)
-        w13_dst = w13[:].rearrange("p a g k -> p (a g k)").bitcast(I32).rearrange("p (a g k) -> p a g k", a=2, g=2 * E)
-        w13_plane_dst = (
-            w13_plane[:].rearrange("p a g k -> p (a g k)").bitcast(I32).rearrange("p (a g k) -> p a g k", a=2, g=2 * E)
-        )
-        for a, words, scales in ((0, w3_words, w3_scales), (1, w1_words, w1_scales)):
+        load_dy(0)
+        load_dy(1)
+        load_dy(2)
+        load_w2(0)
+        load_dy(3)
+        load_first_half("a1", 0)
+        load_first_half("a3", 0)
+        load_w2(1)
+        load_first_half("a1", 1)
+        load_first_half("a3", 1)
+        load_w2(2)
+        load_w2(3)
+        load_second_half("a1")
+        load_second_half("a3")
+        for a, words in ((0, w3_words), (1, w1_words)):
+            nc.sync.dma_start(out=w13_dst[:, a, :, :], in_=words.bitcast(I32).rearrange("e s p k -> p (e s) k"))
+        for a, scales in ((0, w3_scales), (1, w1_scales)):
             scale_src = scales.bitcast(I32).rearrange("e s f k -> f (e s) k")
             for quad in range(4):
                 nc.sync.dma_start(
                     out=w13_plane_dst[32 * quad : 32 * quad + 4, a, :, :],
                     in_=scale_src[4 * quad : 4 * quad + 4, :, :],
                 )
-            nc.sync.dma_start(out=w13_dst[:, a, :, :], in_=words.bitcast(I32).rearrange("e s p k -> p (e s) k"))
-        nc.sync.dma_start(out=w2_dst[:, 2:4, :], in_=w2_src[2:4, 0, :, :].rearrange("e p i -> p e i"))
-        for s in range(2):
-            load_saved("a1", a1, 1, s)
-            load_saved("a3", a3, 1, s)
 
         def gather(t, j0, j1):
             nc.vector.tensor_tensor(
@@ -151,8 +167,12 @@ def tile_moe_bdx_glu_sigmoid_kernel(
             turned[e, s] = dh
 
         def saved_slice(name, e, s):
-            pair, h = divmod(e, 2)
-            return saved[name, pair, s][:, :, C * h : C * (h + 1)].rearrange("p t j -> p j t")
+            if s == 0:
+                half, h = divmod(e, 2)
+                tile = saved[name, 0, half]
+            else:
+                h, tile = e, saved[name, 1]
+            return tile[:, :, C * h : C * (h + 1)].rearrange("p t j -> p j t")
 
         def factors(e, s):
             nc.scalar.activation(saved["sig", e, s][:], saved_slice("a1", e, s), SIGMOID)
@@ -174,8 +194,8 @@ def tile_moe_bdx_glu_sigmoid_kernel(
 
         def quantize_da(e, s):
             da = das[e, s]
-            words = ring.tile([P, 2 * C], U32, name="da_codes", align_bytes=64, bufs=4)
-            scales = ring.tile([P, 2 * C], U8, name="da_scales", align_bytes=64, bufs=4)
+            words = keep.tile([P, 2 * C], U32, name="da_codes_%d%d" % (e, s), align_bytes=64)
+            scales = keep.tile([P, 2 * C], U8, name="da_scales_%d%d" % (e, s), align_bytes=64)
             nc.vector.quantize_mx(
                 out=words[:].bitcast(FP8X4), scales=scales[:], in_=da[:].rearrange("p a j t -> p (a j t)")
             )
@@ -196,7 +216,7 @@ def tile_moe_bdx_glu_sigmoid_kernel(
                             start=(s == 0 and a == 0),
                             stop=(s == 1 and a == 1),
                         )
-            dx_sb = ring.tile([P, 2, C], F32, name="dx_sb")
+            dx_sb = ring.tile([P, 2, C], F32, name="dx_sb", bufs=4)
             nc.scalar.copy(out=dx_sb[:], in_=dx[:])
             return dx_sb
 
@@ -204,7 +224,7 @@ def tile_moe_bdx_glu_sigmoid_kernel(
             for kt in range(2):
                 nc.vector.tensor_copy(windows[kt][:].indirect(offsets[:, 8 * e : 8 * (e + 1)]), dx_sb[:, kt, :])
 
-        steps = [(e, s) for e in range(E) for s in range(2)]
+        steps = [(e, s) for s in range(2) for e in range(E)]
         for t in range(3):
             gather(t, 0, SLOTS)
         gather(3, 0, C)
@@ -214,17 +234,17 @@ def tile_moe_bdx_glu_sigmoid_kernel(
         quantize_g(0)
         interleave(1, nc.vector.tensor_copy)
         first_product(0, 0)
-        first_product(0, 1)
         for e in range(2, E):
             interleave(e, nc.scalar.copy)
         quantize_g(1)
         factors(0, 0)
         factor_products(0, 0)
-        factors(0, 1)
-        factor_products(0, 1)
+        first_product(1, 0)
+        factors(1, 0)
+        factor_products(1, 0)
         quantize_g(2)
         quantize_g(3)
-        factors(1, 0)
+        factors(2, 0)
         dxs = {}
         for i in range(len(steps)):
             e, s = steps[i]
@@ -238,8 +258,9 @@ def tile_moe_bdx_glu_sigmoid_kernel(
             quantize_da(e, s)
             if s == 1:
                 dxs[e] = second_product(e)
-                if e >= 1:
-                    scatter(e - 1, dxs[e - 1])
-        scatter(E - 1, dxs[E - 1])
+            if s == 1 and e == 2:
+                scatter(0, dxs[0])
+        for e in range(1, E):
+            scatter(e, dxs[e])
         for kt in range(2):
             nc.sync.dma_start(out=out[P * kt : P * (kt + 1), :], in_=windows[kt][:])

@@ -94,21 +94,28 @@ def tile_moe_bdx_glu_sigmoid_kernel(
         nc.vector.memset(minus_half[:], -0.5)
         nc.vector.memset(warm[:], 0.0)
         nc.scalar.activation(warm[:], warm[:], SIGMOID)
-        nc.vector.memset(w13_plane[:].rearrange("p a g k -> p (a g k)").bitcast(I32), 0)
         make_identity(nc, ident[:])
         for kt in range(2):
             nc.gpsimd.memset(windows[kt][:], 0.0)
+        nc.gpsimd.memset(w13_plane[:].rearrange("p a g k -> p (a g k)").bitcast(I32), 0)
         for quad in range(4):
             nc.scalar.dma_start(
                 out=w2_plane_dst[32 * quad : 32 * quad + 4, :, :],
                 in_=w2_scale_src[4 * quad : 4 * quad + 4, :, :],
             )
+        for a, scales in ((0, w3_scales), (1, w1_scales)):
+            scale_src = scales.bitcast(I32).rearrange("e s f k -> f (e s) k")
+            for quad in range(4):
+                nc.gpsimd.dma_start(
+                    out=w13_plane_dst[32 * quad : 32 * quad + 4, a, :, :],
+                    in_=scale_src[4 * quad : 4 * quad + 4, :, :],
+                )
         load_dy(0)
         load_dy(1)
         load_dy(2)
-        load_w2(0)
         load_dy(3)
         load_first_half("a1", 0)
+        load_w2(0)
         load_first_half("a3", 0)
         load_w2(1)
         load_first_half("a1", 1)
@@ -119,13 +126,6 @@ def tile_moe_bdx_glu_sigmoid_kernel(
         load_second_half("a3")
         for a, words in ((0, w3_words), (1, w1_words)):
             nc.sync.dma_start(out=w13_dst[:, a, :, :], in_=words.bitcast(I32).rearrange("e s p k -> p (e s) k"))
-        for a, scales in ((0, w3_scales), (1, w1_scales)):
-            scale_src = scales.bitcast(I32).rearrange("e s f k -> f (e s) k")
-            for quad in range(4):
-                nc.sync.dma_start(
-                    out=w13_plane_dst[32 * quad : 32 * quad + 4, a, :, :],
-                    in_=scale_src[4 * quad : 4 * quad + 4, :, :],
-                )
 
         def gather(t, j0, j1):
             nc.vector.tensor_tensor(
@@ -202,13 +202,17 @@ def tile_moe_bdx_glu_sigmoid_kernel(
             codes[e, s] = (words, scales)
 
         def second_product(e):
-            dx = psum.tile([P, 2, C], F32, name="dx")
+            dx_sb = ring.tile([P, 2, C], F32, name="dx_sb", bufs=4)
+            banks = []
             for kt in range(2):
-                for s in range(2):
+                bank = psum.tile([P, C], F32, name="dx%d" % kt, bufs=1)
+                banks.append(bank)
+            for s in range(2):
+                words, scales = codes[e, s]
+                for kt in range(2):
                     for a in range(2):
-                        words, scales = codes[e, s]
                         nc.tensor.matmul_mx(
-                            out=dx[:, kt, :],
+                            out=banks[kt][:],
                             lhsT=w13[:, a, 2 * e + s, 256 * kt : 256 * (kt + 1)].bitcast(FP4X4),
                             lhsT_scale=w13_plane[:, a, 2 * e + s, P * kt : P * (kt + 1)],
                             rhs=words[:, C * a : C * (a + 1)].bitcast(FP8X4),
@@ -216,17 +220,17 @@ def tile_moe_bdx_glu_sigmoid_kernel(
                             start=(s == 0 and a == 0),
                             stop=(s == 1 and a == 1),
                         )
-            dx_sb = ring.tile([P, 2, C], F32, name="dx_sb", bufs=4)
-            nc.scalar.copy(out=dx_sb[:], in_=dx[:])
+            for kt in range(2):
+                nc.scalar.copy(out=dx_sb[:, kt, :], in_=banks[kt][:])
             return dx_sb
 
-        def scatter(e, dx_sb):
-            for kt in range(2):
-                nc.vector.tensor_copy(windows[kt][:].indirect(offsets[:, 8 * e : 8 * (e + 1)]), dx_sb[:, kt, :])
+        def scatter(e, kt, dx_sb):
+            nc.vector.tensor_copy(windows[kt][:].indirect(offsets[:, 8 * e : 8 * (e + 1)]), dx_sb[:, kt, :])
 
         steps = [(e, s) for s in range(2) for e in range(E)]
         for t in range(3):
             gather(t, 0, SLOTS)
+        factors(0, 0)
         gather(3, 0, C)
         gather(3, C, 2 * C)
         interleave(0, nc.vector.tensor_copy)
@@ -234,16 +238,15 @@ def tile_moe_bdx_glu_sigmoid_kernel(
         quantize_g(0)
         interleave(1, nc.vector.tensor_copy)
         first_product(0, 0)
-        for e in range(2, E):
-            interleave(e, nc.scalar.copy)
         quantize_g(1)
-        factors(0, 0)
-        factor_products(0, 0)
         first_product(1, 0)
         factors(1, 0)
-        factor_products(1, 0)
+        interleave(2, nc.vector.tensor_copy)
+        interleave(3, nc.vector.tensor_copy)
+        factor_products(0, 0)
         quantize_g(2)
         quantize_g(3)
+        factor_products(1, 0)
         factors(2, 0)
         dxs = {}
         for i in range(len(steps)):
@@ -258,9 +261,7 @@ def tile_moe_bdx_glu_sigmoid_kernel(
             quantize_da(e, s)
             if s == 1:
                 dxs[e] = second_product(e)
-            if s == 1 and e == 2:
-                scatter(0, dxs[0])
-        for e in range(1, E):
-            scatter(e, dxs[e])
         for kt in range(2):
+            for e in range(E):
+                scatter(e, kt, dxs[e])
             nc.sync.dma_start(out=out[P * kt : P * (kt + 1), :], in_=windows[kt][:])

from contextlib import ExitStack

import concourse.mybir as mybir
from concourse.masks import make_identity

N, T, E, C, H, K = 512, 768, 4, 128, 1024, 256
SLOTS = E * C
P = 128

FLOPS = 2 * SLOTS * H * (N + 2 * K)
BYTES = 4 * (N * T + 2 * H * SLOTS + P * SLOTS + K * T) + 2 * P * SLOTS // 16 + E * (N * H + 2 * H * K) * 17 // 32

F32 = mybir.dt.float32
BF16 = mybir.dt.bfloat16
I32 = mybir.dt.int32
U32 = mybir.dt.uint32
U16 = mybir.dt.uint16
U8 = mybir.dt.uint8
FP8X4 = mybir.dt.float8_e4m3fn_x4
FP4X4 = mybir.dt.float4_e2m1fn_x4
MULT = mybir.AluOpType.mult
SUBTRACT = mybir.AluOpType.subtract
SIGMOID = mybir.ActivationFunctionType.Sigmoid
SQUARE = mybir.ActivationFunctionType.Square


def tile_moe_bdx_glu_sigmoid_kernel(
    tc, dyT, a1, a3, w2_words, w2_scales, w1_words, w1_scales, w3_words, w3_scales, gate, offs, out
):
    nc = tc.nc
    with ExitStack() as ctx:
        keep = ctx.enter_context(tc.tile_pool(name="keep", bufs=1))
        ring = ctx.enter_context(tc.tile_pool(name="ring", bufs=3))
        psum = ctx.enter_context(tc.psum_pool(name="psum", bufs=2))

        offsets = keep.tile([P, SLOTS // 16], U16, name="offsets")
        dy = [keep.tile([P, T], F32, name="dy%d" % t) for t in range(4)]
        gates = keep.tile([P, SLOTS], F32, name="gates")
        g4 = keep.tile([P, 4, SLOTS], F32, name="g4")
        g_bf = keep.tile([P, SLOTS, 4], BF16, name="g_bf", align_bytes=64)
        g_codes = keep.tile([P, SLOTS], U32, name="g_codes", align_bytes=64)
        g_scales = keep.tile([P, SLOTS], U8, name="g_scales", align_bytes=64)
        w2 = keep.tile([P, E, 2 * H], U8, name="w2", align_bytes=64)
        w2_plane = keep.tile([P, E, H], U8, name="w2_plane", align_bytes=64)
        w13 = keep.tile([P, 2, 2 * E, 2 * K], U8, name="w13", align_bytes=64)
        w13_plane = keep.tile([P, 2, 2 * E, K], U8, name="w13_plane", align_bytes=64)
        ident = keep.tile([P, P], F32, name="ident")
        windows = [keep.tile([P, T], F32, name="window%d" % kt) for kt in range(2)]
        warm = keep.tile([P, 1], F32, name="warm")
        minus_half = keep.tile([P, 1], F32, name="minus_half")
        saved = {}
        for name in ("a1", "a3"):
            for half in range(2):
                saved[name, 0, half] = keep.tile([P, 4, 2 * C], F32, name="%s_0%d" % (name, half))
            saved[name, 1] = keep.tile([P, 4, SLOTS], F32, name="%s_1" % name)
        for name in ("sig", "sq", "nq"):
            for e in range(E):
                for s in range(2):
                    saved[name, e, s] = keep.tile([P, C, 4], F32, name="%s_%d%d" % (name, e, s))

        sources = {"a1": a1, "a3": a3}

        def load_first_half(name, half):
            nc.sync.dma_start(
                out=saved[name, 0, half][:],
                in_=sources[name][0:512, 2 * C * half : 2 * C * (half + 1)].rearrange("(p t) j -> p t j", t=4),
            )

        def load_second_half(name):
            nc.sync.dma_start(
                out=saved[name, 1][:], in_=sources[name][512:1024, :].rearrange("(p t) j -> p t j", t=4)
            )

        w2_src = w2_words.bitcast(I32)
        w2_scale_src = w2_scales.bitcast(I32).rearrange("e s f i -> f (e s) i")
        w2_dst = w2[:].rearrange("p e i -> p (e i)").bitcast(I32).rearrange("p (e i) -> p e i", e=E)
        w2_plane_dst = w2_plane[:].rearrange("p e i -> p (e i)").bitcast(I32).rearrange("p (e i) -> p e i", e=E)
        w13_dst = w13[:].rearrange("p a g k -> p (a g k)").bitcast(I32).rearrange("p (a g k) -> p a g k", a=2, g=2 * E)
        w13_plane_dst = (
            w13_plane[:].rearrange("p a g k -> p (a g k)").bitcast(I32).rearrange("p (a g k) -> p a g k", a=2, g=2 * E)
        )

        def load_w2(e):
            nc.sync.dma_start(out=w2_dst[:, e, :], in_=w2_src[e, 0, :, :])

        dy_rows = dyT.rearrange("(p t) j -> p t j", t=4)

        def load_dy(t):
            nc.sync.dma_start(out=dy[t][:], in_=dy_rows[:, t, :])

        nc.sync.dma_start(offsets[:], offs)
        nc.scalar.dma_start(out=gates[:], in_=gate[0:P, :])
        nc.vector.memset(w2_plane[:].rearrange("p e i -> p (e i)").bitcast(I32), 0)
        nc.vector.memset(minus_half[:], -0.5)
        nc.vector.memset(warm[:], 0.0)
        nc.scalar.activation(warm[:], warm[:], SIGMOID)
        make_identity(nc, ident[:])
        for kt in range(2):
            nc.gpsimd.memset(windows[kt][:], 0.0)
        nc.gpsimd.memset(w13_plane[:].rearrange("p a g k -> p (a g k)").bitcast(I32), 0)
        for quad in range(4):
            nc.scalar.dma_start(
                out=w2_plane_dst[32 * quad : 32 * quad + 4, :, :],
                in_=w2_scale_src[4 * quad : 4 * quad + 4, :, :],
            )
        for a, scales in ((0, w3_scales), (1, w1_scales)):
            scale_src = scales.bitcast(I32).rearrange("e s f k -> f (e s) k")
            for quad in range(4):
                nc.gpsimd.dma_start(
                    out=w13_plane_dst[32 * quad : 32 * quad + 4, a, :, :],
                    in_=scale_src[4 * quad : 4 * quad + 4, :, :],
                )
        load_dy(0)
        load_dy(1)
        load_dy(2)
        load_dy(3)
        load_first_half("a1", 0)
        load_w2(0)
        load_first_half("a3", 0)
        load_w2(1)
        load_first_half("a1", 1)
        load_first_half("a3", 1)
        load_w2(2)
        load_w2(3)
        load_second_half("a1")
        load_second_half("a3")
        for a, words in ((0, w3_words), (1, w1_words)):
            nc.sync.dma_start(out=w13_dst[:, a, :, :], in_=words.bitcast(I32).rearrange("e s p k -> p (e s) k"))

        def gather(t, j0, j1):
            nc.vector.tensor_tensor(
                g4[:, t, j0:j1], dy[t][:].indirect(offsets[:, j0 // 16 : j1 // 16]), gates[:, j0:j1], MULT
            )

        def interleave(e, copy):
            copy(
                out=g_bf[:, C * e : C * (e + 1), :], in_=g4[:, :, C * e : C * (e + 1)].rearrange("p t j -> p j t")
            )

        def quantize_g(e):
            cols = slice(C * e, C * (e + 1))
            nc.vector.quantize_mx(
                out=g_codes[:, cols].bitcast(FP8X4),
                scales=g_scales[:, cols],
                in_=g_bf[:, cols, :].rearrange("p j t -> p (j t)"),
            )

        turned = {}
        codes = {}

        def first_product(e, s):
            dhT = psum.tile([P, 512], F32, name="dhT")
            nc.tensor.matmul_mx(
                out=dhT[:],
                lhsT=g_codes[:, C * e : C * (e + 1)].bitcast(FP8X4),
                lhsT_scale=g_scales[:, C * e : C * (e + 1)],
                rhs=w2[:, e, 1024 * s : 1024 * (s + 1)].bitcast(FP4X4),
                rhs_scale=w2_plane[:, e, 512 * s : 512 * (s + 1)],
                start=True,
                stop=True,
            )
            dhT_sb = ring.tile([P, 4, P], F32, name="dhT_sb")
            nc.scalar.copy(out=dhT_sb[:], in_=dhT[:].rearrange("j (m t) -> j t m", t=4))
            dh = psum.tile([P, 4, P], F32, name="dh", bufs=4)
            for t in range(4):
                nc.tensor.transpose(dh[:, t, :], dhT_sb[:, t, :], ident[:])
            turned[e, s] = dh

        def saved_slice(name, e, s):
            if s == 0:
                half, h = divmod(e, 2)
                tile = saved[name, 0, half]
            else:
                h, tile = e, saved[name, 1]
            return tile[:, :, C * h : C * (h + 1)].rearrange("p t j -> p j t")

        def factors(e, s):
            nc.scalar.activation(saved["sig", e, s][:], saved_slice("a1", e, s), SIGMOID)
            nc.scalar.activation(saved["sq", e, s][:], saved["sig", e, s][:], SQUARE, bias=minus_half[:])

        def factor_products(e, s):
            nc.vector.scalar_tensor_tensor(
                saved["nq", e, s][:], saved["sq", e, s][:], 0.25, saved_slice("a3", e, s), SUBTRACT, MULT
            )

        das = {}

        def product_da(e, s):
            da = ring.tile([P, 2, C, 4], BF16, name="da", align_bytes=64)
            dh = turned[e, s][:].rearrange("p t j -> p j t")
            nc.vector.tensor_tensor(da[:, 0, :, :], dh, saved["sig", e, s][:], MULT)
            nc.vector.scalar_tensor_tensor(da[:, 1, :, :], dh, -1.0, saved["nq", e, s][:], MULT, MULT)
            das[e, s] = da

        def quantize_da(e, s):
            da = das[e, s]
            words = keep.tile([P, 2 * C], U32, name="da_codes_%d%d" % (e, s), align_bytes=64)
            scales = keep.tile([P, 2 * C], U8, name="da_scales_%d%d" % (e, s), align_bytes=64)
            nc.vector.quantize_mx(
                out=words[:].bitcast(FP8X4), scales=scales[:], in_=da[:].rearrange("p a j t -> p (a j t)")
            )
            codes[e, s] = (words, scales)

        def second_product(e):
            dx_sb = ring.tile([P, 2, C], F32, name="dx_sb", bufs=4)
            banks = []
            for kt in range(2):
                bank = psum.tile([P, C], F32, name="dx%d" % kt, bufs=1)
                banks.append(bank)
            for s in range(2):
                words, scales = codes[e, s]
                for kt in range(2):
                    for a in range(2):
                        nc.tensor.matmul_mx(
                            out=banks[kt][:],
                            lhsT=w13[:, a, 2 * e + s, 256 * kt : 256 * (kt + 1)].bitcast(FP4X4),
                            lhsT_scale=w13_plane[:, a, 2 * e + s, P * kt : P * (kt + 1)],
                            rhs=words[:, C * a : C * (a + 1)].bitcast(FP8X4),
                            rhs_scale=scales[:, C * a : C * (a + 1)],
                            start=(s == 0 and a == 0),
                            stop=(s == 1 and a == 1),
                        )
            for kt in range(2):
                nc.scalar.copy(out=dx_sb[:, kt, :], in_=banks[kt][:])
            return dx_sb

        def scatter(e, kt, dx_sb):
            nc.vector.tensor_copy(windows[kt][:].indirect(offsets[:, 8 * e : 8 * (e + 1)]), dx_sb[:, kt, :])

        steps = [(e, s) for s in range(2) for e in range(E)]
        for t in range(3):
            gather(t, 0, SLOTS)
        factors(0, 0)
        gather(3, 0, C)
        gather(3, C, 2 * C)
        interleave(0, nc.vector.tensor_copy)
        gather(3, 2 * C, SLOTS)
        quantize_g(0)
        interleave(1, nc.vector.tensor_copy)
        first_product(0, 0)
        quantize_g(1)
        first_product(1, 0)
        factors(1, 0)
        interleave(2, nc.vector.tensor_copy)
        interleave(3, nc.vector.tensor_copy)
        factor_products(0, 0)
        quantize_g(2)
        quantize_g(3)
        factor_products(1, 0)
        factors(2, 0)
        dxs = {}
        for i in range(len(steps)):
            e, s = steps[i]
            if i + 2 < len(steps):
                first_product(*steps[i + 2])
            if i + 3 < len(steps):
                factors(*steps[i + 3])
            product_da(e, s)
            if i + 2 < len(steps):
                factor_products(*steps[i + 2])
            quantize_da(e, s)
            if s == 1:
                dxs[e] = second_product(e)
        for kt in range(2):
            for e in range(E):
                scatter(e, kt, dxs[e])
            nc.sync.dma_start(out=out[P * kt : P * (kt + 1), :], in_=windows[kt][:])
